import numpy as np
import ml_dtypes


def mxq(x, axis, fmt="e4m3"):
    dtype, down = {"e4m3": (ml_dtypes.float8_e4m3fn, 7), "e5m2": (ml_dtypes.float8_e5m2, 14)}[fmt]
    v = np.moveaxis(np.asarray(x, np.float32).astype(ml_dtypes.bfloat16).astype(np.float64), axis, -1)
    blocks = v.reshape(v.shape[:-1] + (-1, 32))
    amax = np.abs(blocks).max(-1, keepdims=True)
    byte = np.maximum(np.where(amax > 0, np.frexp(amax)[1] - 1 + 127, 0) - down, 1)
    scale = np.exp2(byte - 127.0)
    codes = (blocks / scale).astype(np.float32).astype(dtype).astype(np.float64)
    return np.moveaxis((codes * scale).reshape(v.shape), -1, axis)


WIDE = False


def mx_kscale(k):
    if not WIDE:
        return np.ones(k)
    levels = np.array([10, -10, 5, -5, 0])
    if k % 512:
        return np.exp2(np.random.permutation(np.resize(levels, k // 32))).repeat(32)
    a = np.empty((k // 512, 16))
    for p in range(k // 512):
        a[p, :8] = np.random.permutation(np.resize(levels, 8))
        for g in range(8):
            far = levels[np.abs(levels - a[p, g]) >= 10]
            a[p, g + 8] = far[np.random.randint(len(far))]
    return np.exp2(a.ravel()).repeat(32)


def f64(x):
    return np.asarray(x).astype(np.float64)


def striped(idx):
    return np.tile(idx.reshape(-1, 16).T, (8, 1)).astype(np.uint16)


def unstriped(offs):
    return offs[:16].T.reshape(-1).astype(np.int64)


E2M1 = np.array([0.0, 0.5, 1.0, 1.5, 2.0, 3.0, 4.0, 6.0, -0.0, -0.5, -1.0, -1.5, -2.0, -3.0, -4.0, -6.0])


def pack_weight(w, fmt):
    k, n = w.shape
    w = f64(np.asarray(w, np.float32).astype(ml_dtypes.bfloat16)).reshape(k // 32, 32, n)
    amax = np.abs(w).max(1)
    if fmt == "e4m3":
        byte = np.frexp(amax)[1] - 1 + 127 - 7
    else:
        mant, ex = np.frexp(amax / 6.0)
        byte = np.where(mant > 0.5, ex, ex - 1) + 127
    byte = np.clip(np.where(amax > 0, byte, 1), 1, 254)
    scaled = (w * np.exp2(127.0 - byte)[:, None, :]).reshape(k, n).astype(np.float32)
    by_word = np.ascontiguousarray(scaled.reshape(k // 512, 128, 4, n).transpose(0, 1, 3, 2))
    if fmt == "e4m3":
        words = by_word.astype(ml_dtypes.float8_e4m3fn).view(np.uint8)
    else:
        c = by_word.astype(ml_dtypes.float4_e2m1fn).view(np.uint8) & 0xF
        words = (c[..., 0::2] | (c[..., 1::2] << 4)).reshape(k // 512, 128, 2 * n)
    return np.ascontiguousarray(words), np.ascontiguousarray(byte.astype(np.uint8).reshape(k // 512, 16, n))


def unpack_weight(words, scales, fmt):
    g, _, n = scales.shape
    words = np.ascontiguousarray(words).reshape(g, 128, n, -1)
    if fmt == "e4m3":
        vals = words.view(ml_dtypes.float8_e4m3fn).astype(np.float64)
    else:
        nib = np.empty((g, 128, n, 4), np.uint8)
        nib[..., 0::2] = words & 0xF
        nib[..., 1::2] = words >> 4
        vals = E2M1[nib]
    vals = vals * np.repeat(np.exp2(scales.astype(np.float64) - 127.0), 8, axis=1)[..., None]
    return vals.transpose(0, 1, 3, 2).reshape(g * 512, n)


def gelu(v):
    return 0.5 * v * (1.0 + np.tanh(np.sqrt(2.0 / np.pi) * (v + 0.044715 * v**3)))


K, T, S, H, P, N = 1536, 4096, 1024, 1024, 512, 640

def setup_inputs():
    n = np.random.standard_normal
    s = mx_kscale(K)[:, None]
    u = mx_kscale(H)[:, None]
    d = {}
    d["tab_words"], d["tab_scales"] = pack_weight(n((K, T)) * s, "e2m1")
    d["offs"] = striped(np.random.permutation(T)[:S])
    d["pos1"] = striped(np.random.permutation(S)[:P])
    d["pos2"] = striped(np.random.permutation(S)[:P])
    d["w1"] = (n((K, H)) / K**0.5 / s).astype(np.float32)
    d["gain"] = (2.0 * np.exp(0.3 * n(H)) * u[:, 0]).astype(np.float32)
    d["base"] = (np.exp(0.3 * n(H)) * u[:, 0]**2).astype(np.float32)
    d["w2_words"], d["w2_scales"] = pack_weight(n((H, N)) / H**0.5 / u, "e2m1")
    d["thr"] = (1.5 * n(N)).astype(np.float32)
    return d

def reference(tab_words, tab_scales, offs, pos1, pos2, w1, gain, base, w2_words, w2_scales, thr):
    v = unpack_weight(tab_words, tab_scales, "e2m1")[:, unstriped(offs)]
    w2 = unpack_weight(w2_words, w2_scales, "e2m1")
    h = f64(gain)[:, None] * (mxq(f64(w1), 0, "e4m3").T @ v)
    windward = h[:, unstriped(pos1)]
    lee = h[:, unstriped(pos2)]
    z = np.sqrt(np.abs(windward * lee) + f64(base)[:, None])
    y = w2.T @ mxq(z, 0, "e4m3")
    return np.abs(y - f64(thr)[:, None])

@@ -1,0 +1,253 @@
+from contextlib import ExitStack
+
+import concourse.mybir as mybir
+
+K, T, S, H, NP, N = 1536, 4096, 1024, 1024, 512, 640
+FLOPS = 2 * K * H * S + 2 * H * N * NP
+
+F32 = mybir.dt.float32
+BF16 = mybir.dt.bfloat16
+I32 = mybir.dt.int32
+U32 = mybir.dt.uint32
+U16 = mybir.dt.uint16
+U8 = mybir.dt.uint8
+FP8X4 = mybir.dt.float8_e4m3fn_x4
+FP4X4 = mybir.dt.float4_e2m1fn_x4
+ACT = mybir.ActivationFunctionType
+ALU = mybir.AluOpType
+
+P = 128
+PACK = 4
+KP = P * PACK
+A1 = K // KP
+A2 = H // KP
+BANK = 512
+
+
+def tile_list_fog_pair_yield_kernel(tc, tab_words, tab_scales, offs, pos1, pos2, w1, gain, base, w2_words, w2_scales, thr, out):
+    nc = tc.nc
+    with ExitStack() as ctx:
+        lists = ctx.enter_context(tc.tile_pool(name="lists", bufs=1))
+        keep = ctx.enter_context(tc.tile_pool(name="keep", bufs=1))
+        stage = ctx.enter_context(tc.tile_pool(name="stage", bufs=3))
+        ring = ctx.enter_context(tc.tile_pool(name="ring", bufs=5))
+        psum = ctx.enter_context(tc.psum_pool(name="psum", bufs=8))
+
+        offs_t = lists.tile([P, S // 16], U16, name="offs_t")
+        pos1_t = lists.tile([P, NP // 16], U16, name="pos1_t")
+        pos2_t = lists.tile([P, NP // 16], U16, name="pos2_t")
+        nc.sync.dma_start(offs_t[:], offs)
+        nc.sync.dma_start(pos1_t[:], pos1)
+        nc.sync.dma_start(pos2_t[:], pos2)
+
+        sc_win = keep.tile([P, T], U8, name="sc_win")
+        nc.vector.memset(sc_win[0:16, :].bitcast(I32), 0)
+        nc.vector.memset(sc_win[64:P, :].bitcast(I32), 0)
+        nc.scalar.dma_start(sc_win[16:64, :].bitcast(I32), tab_scales.rearrange("a q t -> q a t").bitcast(I32))
+
+        warm_in = keep.tile([P, 1], F32, name="warm_in")
+        warm_out = keep.tile([P, 1], F32, name="warm_out")
+        nc.vector.memset(warm_in[:], 1.0)
+        nc.scalar.activation(warm_out[:], warm_in[:], ACT.Sqrt)
+
+        v_scales = keep.tile([P, A1 * S], U8, name="v_scales", align_bytes=64)
+        nc.vector.memset(v_scales[:].bitcast(I32), 0)
+        w2_sc = keep.tile([P, A2 * N], U8, name="w2_sc", align_bytes=64)
+        nc.vector.memset(w2_sc[:].bitcast(I32), 0)
+
+        gain_t = keep.tile([P, A2, PACK], F32, name="gain_t")
+        base_t = keep.tile([P, A2, PACK], F32, name="base_t")
+        thr_t = keep.tile([P, N // P], F32, name="thr_t")
+        nc.gpsimd.dma_start(gain_t[:], gain.rearrange("(b p t) -> p b t", p=P, t=PACK))
+        nc.gpsimd.dma_start(base_t[:], base.rearrange("(b p t) -> p b t", p=P, t=PACK))
+        for q in range(4):
+            nc.gpsimd.dma_start(
+                w2_sc[32 * q : 32 * q + 4, :].bitcast(I32).rearrange("r (a c) -> r a c", a=A2),
+                w2_scales[:, 4 * q : 4 * q + 4, :].rearrange("a r c -> r a c").bitcast(I32),
+            )
+        with nc.allow_non_contiguous_dma(reason="one threshold for each partition"):
+            nc.gpsimd.dma_start(thr_t[:], thr.rearrange("(i p) -> p i", p=P))
+
+        tab_win = [keep.tile([P, T], U16, name="tab_win", tag="slot1%d" % a, align_bytes=64) for a in range(A1)]
+        v_words = [keep.tile([P, S], U16, name="v_words%d" % a, align_bytes=64) for a in range(A1)]
+        w1_codes = {}
+        w1_sc = {}
+        raw = {}
+
+        def load_tab(a):
+            nc.sync.dma_start(tab_win[a][:].bitcast(I32), tab_words[a].bitcast(I32))
+
+        def load_w1(b, a):
+            raw[b, a] = keep.tile([P, PACK, KP], F32, name="raw", tag="slot%d%d" % (b, a), align_bytes=64)
+            nc.sync.dma_start(raw[b, a][:], w1[KP * a : KP * (a + 1), KP * b : KP * (b + 1)].rearrange("(p j) c -> p j c", j=PACK))
+
+        def quant_w1(b, a, m_vec, cuts=((0, KP),)):
+            wb = stage.tile([P, PACK * KP], BF16, name="wb", align_bytes=64)
+            dst = wb[:].rearrange("p (t m j) -> p m j t", t=PACK, j=PACK)
+            src = raw[b, a][:].rearrange("p j (m t) -> p m j t", t=PACK)
+            if m_vec < P:
+                nc.scalar.copy(dst[:, m_vec:P], src[:, m_vec:P])
+            if m_vec > 0:
+                nc.vector.tensor_copy(dst[:, 0:m_vec], src[:, 0:m_vec])
+            w1_codes[b, a] = keep.tile([P, KP], U32, name="w1_codes%d%d" % (b, a), align_bytes=64)
+            w1_sc[b, a] = keep.tile([P, KP], U8, name="w1_sc%d%d" % (b, a), align_bytes=64)
+            for lo, hi in cuts:
+                nc.vector.quantize_mx(out=w1_codes[b, a][:, lo:hi].bitcast(FP8X4), scales=w1_sc[b, a][:, lo:hi], in_=wb[:, PACK * lo : PACK * hi])
+
+        def gather_tab(a):
+            nc.vector.tensor_copy(v_words[a][:], tab_win[a][:].indirect(offs_t[:]))
+
+        load_tab(0)
+        load_tab(1)
+        load_w1(0, 0)
+        load_tab(2)
+        load_w1(0, 1)
+        load_w1(0, 2)
+
+        sc_got = keep.tile([P, S], U8, name="sc_got")
+        nc.vector.tensor_copy(sc_got[:], sc_win[:].indirect(offs_t[:]))
+        for q in range(4):
+            nc.scalar.dma_start(
+                v_scales[32 * q : 32 * q + 4, :].bitcast(I32).rearrange("r (a c) -> r a c", a=A1),
+                sc_got[16 + 4 * A1 * q : 16 + 4 * A1 * (q + 1), :].bitcast(I32),
+            )
+
+        gather_tab(0)
+        gather_tab(1)
+        quant_w1(0, 0, 0)
+        load_w1(1, 0)
+        gather_tab(2)
+        quant_w1(0, 1, 52)
+        load_w1(1, 1)
+        quant_w1(0, 2, 84, ((0, P), (P, 2 * P), (2 * P, KP)))
+        load_w1(1, 2)
+
+        h = {}
+
+        def stage1(b, t):
+            h[b, t] = keep.tile([P, S], F32, name="h%d%d" % (b, t))
+            for half in range(S // BANK):
+                cols = slice(BANK * half, BANK * (half + 1))
+                acc = psum.tile([P, BANK], F32, name="acc", tag="acc")
+                for a in range(A1):
+                    nc.tensor.matmul_mx(
+                        out=acc[:],
+                        lhsT=w1_codes[b, a][:, P * t : P * (t + 1)].bitcast(FP8X4),
+                        lhsT_scale=w1_sc[b, a][:, P * t : P * (t + 1)],
+                        rhs=v_words[a][:, cols].bitcast(FP4X4),
+                        rhs_scale=v_scales[:, S * a + BANK * half : S * a + BANK * (half + 1)],
+                        start=(a == 0),
+                        stop=(a == A1 - 1),
+                    )
+                nc.scalar.activation(h[b, t][:, cols], acc[:], ACT.Abs, scale=gain_t[:, b, t : t + 1])
+
+        z_rows = [keep.tile([P, PACK, NP], BF16, name="z_rows%d" % b) for b in range(A2)]
+        z_codes = [keep.tile([P, NP], U32, name="z_codes0", align_bytes=64)]
+        z_sc = [keep.tile([P, NP], U8, name="z_sc0", align_bytes=64)]
+
+        prods = {}
+
+        def pairs(b, t):
+            wind = ring.tile([P, NP], F32, name="wind")
+            prods[b, t] = ring.tile([P, NP], F32, name="prod")
+            parts = [(0, NP // 2), (NP // 2, NP)]
+            for lo, hi in parts:
+                nc.vector.tensor_copy(wind[:, lo:hi], h[b, t][:].indirect(pos1_t[:, lo // 16 : hi // 16]))
+            for lo, hi in parts:
+                nc.vector.tensor_tensor(prods[b, t][:, lo:hi], h[b, t][:].indirect(pos2_t[:, lo // 16 : hi // 16]), wind[:, lo:hi], ALU.mult)
+
+        def root(b, t):
+            nc.scalar.activation(z_rows[b][:, t, :], prods[b, t][:], ACT.Sqrt, bias=base_t[:, b, t : t + 1])
+
+        def quant_z(b, copy):
+            zi = stage.tile([P, NP * PACK], BF16, name="zi", align_bytes=64)
+            copy(zi[:].rearrange("p (c i t) -> p c t i", i=4, t=PACK), z_rows[b][:].rearrange("p t (c i) -> p c t i", i=4))
+            nc.vector.quantize_mx(out=z_codes[b][:].bitcast(FP8X4), scales=z_sc[b][:], in_=zi[:])
+
+        stage1(0, 0)
+        stage1(0, 1)
+        pairs(0, 0)
+        quant_w1(1, 0, 0)
+        w2_t = keep.tile([P, A2, 2 * N], U8, name="w2_t", tag="slot01", align_bytes=64)
+        nc.sync.dma_start(w2_t[:].bitcast(I32), w2_words.rearrange("a p c -> p a c").bitcast(I32))
+        pairs(0, 1)
+        stage1(0, 2)
+        quant_w1(1, 1, 0)
+        pairs(0, 2)
+        quant_w1(1, 2, 64)
+        stage1(0, 3)
+        pairs(0, 3)
+        root(0, 0)
+        root(0, 1)
+        stage1(1, 0)
+        root(0, 2)
+        pairs(1, 0)
+        stage1(1, 1)
+        root(0, 3)
+        pairs(1, 1)
+        stage1(1, 2)
+        quant_z(0, nc.scalar.copy)
+        root(1, 0)
+        HALF = NP // 2
+        wind_last = {}
+        prod_last = {}
+
+        def pick(t, part, slot):
+            wind_last[t, part] = keep.tile([P, HALF], F32, name="wind_last", tag="wind_last%d" % slot)
+            nc.vector.tensor_copy(wind_last[t, part][:], h[1, t][:].indirect(pos1_t[:, HALF // 16 * part : HALF // 16 * (part + 1)]))
+
+        def times(t, part):
+            prod_last[t, part] = keep.tile([P, HALF], F32, name="prod_last%d%d" % (t, part))
+            nc.vector.tensor_tensor(prod_last[t, part][:], h[1, t][:].indirect(pos2_t[:, HALF // 16 * part : HALF // 16 * (part + 1)]), wind_last[t, part][:], ALU.mult)
+
+        def root_part(t, part):
+            nc.scalar.activation(z_rows[1][:, t, HALF * part : HALF * (part + 1)], prod_last[t, part][:], ACT.Sqrt, bias=base_t[:, 1, t : t + 1])
+
+        zl_codes = [keep.tile([P, HALF], U32, name="zl_codes%d" % part, align_bytes=64) for part in range(2)]
+        zl_sc = [keep.tile([P, HALF], U8, name="zl_sc%d" % part, align_bytes=64) for part in range(2)]
+
+        def quant_part(part, copy):
+            zi = keep.tile([P, HALF * PACK], BF16, name="zil%d" % part, align_bytes=64)
+            copy(zi[:].rearrange("p (c i t) -> p c t i", i=4, t=PACK), z_rows[1][:, :, HALF * part : HALF * (part + 1)].rearrange("p t (c i) -> p c t i", i=4))
+            nc.vector.quantize_mx(out=zl_codes[part][:].bitcast(FP8X4), scales=zl_sc[part][:], in_=zi[:])
+
+        def stage2(part):
+            for i in range(N // P):
+                acc = psum.tile([P, BANK], F32, name="acc", tag="acc")
+                for b in range(A2):
+                    for c in range(HALF // P):
+                        if b == 0:
+                            codes, sc, lo = z_codes[0], z_sc[0], HALF * part + P * c
+                        else:
+                            codes, sc, lo = zl_codes[part], zl_sc[part], P * c
+                        nc.tensor.matmul_mx(
+                            out=acc[:, P * c : P * (c + 1)],
+                            lhsT=w2_t[:, b, 2 * P * i : 2 * P * (i + 1)].bitcast(FP4X4),
+                            lhsT_scale=w2_sc[:, N * b + P * i : N * b + P * (i + 1)],
+                            rhs=codes[:, lo : lo + P].bitcast(FP8X4),
+                            rhs_scale=sc[:, lo : lo + P],
+                            start=(b == 0 and c == 0),
+                            stop=(b == A2 - 1 and c == HALF // P - 1),
+                        )
+                res = keep.tile([P, HALF], F32, name="res%d%d" % (part, i))
+                nc.scalar.activation(res[:], acc[:, 0:HALF], ACT.Abs, bias=thr_t[:, i : i + 1], scale=-1.0)
+                nc.sync.dma_start(out[P * i : P * (i + 1), HALF * part : HALF * (part + 1)], res[:])
+
+        stage1(1, 3)
+        root(1, 1)
+        pick(2, 0, 0)
+        pick(3, 0, 1)
+        times(2, 0)
+        times(3, 0)
+        pick(3, 1, 0)
+        pick(2, 1, 1)
+        root_part(2, 0)
+        root_part(3, 0)
+        times(3, 1)
+        times(2, 1)
+        quant_part(0, nc.scalar.copy)
+        root_part(3, 1)
+        root_part(2, 1)
+        quant_part(1, nc.vector.tensor_copy)
+        stage2(0)
+        stage2(1)

@@ -37,13 +37,14 @@ def tile_list_fog_pair_yield_kernel(tc, tab_words, tab_scales, offs, pos1, pos2,
         pos1_t = lists.tile([P, NP // 16], U16, name="pos1_t")
         pos2_t = lists.tile([P, NP // 16], U16, name="pos2_t")
         nc.sync.dma_start(offs_t[:], offs)
+
+        sc_win = keep.tile([P, T], U8, name="sc_win", tag="slot01", align_bytes=64)
+        for a in range(A1):
+            nc.sync.dma_start(sc_win[16 + a : 64 : A1, :].bitcast(I32), tab_scales[a].bitcast(I32))
         nc.sync.dma_start(pos1_t[:], pos1)
         nc.sync.dma_start(pos2_t[:], pos2)
-
-        sc_win = keep.tile([P, T], U8, name="sc_win")
         nc.vector.memset(sc_win[0:16, :].bitcast(I32), 0)
         nc.vector.memset(sc_win[64:P, :].bitcast(I32), 0)
-        nc.scalar.dma_start(sc_win[16:64, :].bitcast(I32), tab_scales.rearrange("a q t -> q a t").bitcast(I32))
 
         warm_in = keep.tile([P, 1], F32, name="warm_in")
         warm_out = keep.tile([P, 1], F32, name="warm_out")
@@ -68,17 +69,18 @@ def tile_list_fog_pair_yield_kernel(tc, tab_words, tab_scales, offs, pos1, pos2,
         with nc.allow_non_contiguous_dma(reason="one threshold for each partition"):
             nc.gpsimd.dma_start(thr_t[:], thr.rearrange("(i p) -> p i", p=P))
 
-        tab_win = [keep.tile([P, T], U16, name="tab_win", tag="slot1%d" % a, align_bytes=64) for a in range(A1)]
+        tab_win = [keep.tile([P, T], U16, name="tab_win", tag="slot_tab%d" % a, align_bytes=64) for a in range(A1)]
         v_words = [keep.tile([P, S], U16, name="v_words%d" % a, align_bytes=64) for a in range(A1)]
         w1_codes = {}
         w1_sc = {}
         raw = {}
+        raw_slot = {(0, 0): "slot00", (0, 1): "slot01", (0, 2): "slot_tab0", (1, 0): "slot_tab1", (1, 1): "slot00", (1, 2): "slot_tab2"}
 
         def load_tab(a):
             nc.sync.dma_start(tab_win[a][:].bitcast(I32), tab_words[a].bitcast(I32))
 
         def load_w1(b, a):
-            raw[b, a] = keep.tile([P, PACK, KP], F32, name="raw", tag="slot%d%d" % (b, a), align_bytes=64)
+            raw[b, a] = keep.tile([P, PACK, KP], F32, name="raw", tag=raw_slot[b, a], align_bytes=64)
             nc.sync.dma_start(raw[b, a][:], w1[KP * a : KP * (a + 1), KP * b : KP * (b + 1)].rearrange("(p j) c -> p j c", j=PACK))
 
         def quant_w1(b, a, m_vec, cuts=((0, KP),)):
@@ -101,8 +103,6 @@ def tile_list_fog_pair_yield_kernel(tc, tab_words, tab_scales, offs, pos1, pos2,
         load_tab(1)
         load_w1(0, 0)
         load_tab(2)
-        load_w1(0, 1)
-        load_w1(0, 2)
 
         sc_got = keep.tile([P, S], U8, name="sc_got")
         nc.vector.tensor_copy(sc_got[:], sc_win[:].indirect(offs_t[:]))
@@ -112,15 +112,17 @@ def tile_list_fog_pair_yield_kernel(tc, tab_words, tab_scales, offs, pos1, pos2,
                 sc_got[16 + 4 * A1 * q : 16 + 4 * A1 * (q + 1), :].bitcast(I32),
             )
 
+        load_w1(0, 1)
         gather_tab(0)
+        load_w1(0, 2)
         gather_tab(1)
-        quant_w1(0, 0, 0)
         load_w1(1, 0)
-        gather_tab(2)
-        quant_w1(0, 1, 52)
+        quant_w1(0, 0, 0)
         load_w1(1, 1)
-        quant_w1(0, 2, 84, ((0, P), (P, 2 * P), (2 * P, KP)))
+        gather_tab(2)
         load_w1(1, 2)
+        quant_w1(0, 1, 52)
+        quant_w1(0, 2, 84, ((0, P), (P, 2 * P), (2 * P, KP)))
 
         h = {}
 
@@ -196,20 +198,26 @@ def tile_list_fog_pair_yield_kernel(tc, tab_words, tab_scales, offs, pos1, pos2,
             wind_last[t, part] = keep.tile([P, HALF], F32, name="wind_last", tag="wind_last%d" % slot)
             nc.vector.tensor_copy(wind_last[t, part][:], h[1, t][:].indirect(pos1_t[:, HALF // 16 * part : HALF // 16 * (part + 1)]))
 
-        def times(t, part):
             prod_last[t, part] = keep.tile([P, HALF], F32, name="prod_last%d%d" % (t, part))
-            nc.vector.tensor_tensor(prod_last[t, part][:], h[1, t][:].indirect(pos2_t[:, HALF // 16 * part : HALF // 16 * (part + 1)]), wind_last[t, part][:], ALU.mult)
 
-        def root_part(t, part):
-            nc.scalar.activation(z_rows[1][:, t, HALF * part : HALF * (part + 1)], prod_last[t, part][:], ACT.Sqrt, bias=base_t[:, 1, t : t + 1])
+        def times(t, part, lo, hi):
+            first = HALF * part
+            nc.vector.tensor_tensor(prod_last[t, part][:, lo:hi], h[1, t][:].indirect(pos2_t[:, (first + lo) // 16 : (first + hi) // 16]), wind_last[t, part][:, lo:hi], ALU.mult)
+
+        def root_part(t, part, lo, hi):
+            first = HALF * part
+            nc.scalar.activation(z_rows[1][:, t, first + lo : first + hi], prod_last[t, part][:, lo:hi], ACT.Sqrt, bias=base_t[:, 1, t : t + 1])
 
         zl_codes = [keep.tile([P, HALF], U32, name="zl_codes%d" % part, align_bytes=64) for part in range(2)]
         zl_sc = [keep.tile([P, HALF], U8, name="zl_sc%d" % part, align_bytes=64) for part in range(2)]
+        zl = [keep.tile([P, HALF * PACK], BF16, name="zl%d" % part, align_bytes=64) for part in range(2)]
 
-        def quant_part(part, copy):
-            zi = keep.tile([P, HALF * PACK], BF16, name="zil%d" % part, align_bytes=64)
-            copy(zi[:].rearrange("p (c i t) -> p c t i", i=4, t=PACK), z_rows[1][:, :, HALF * part : HALF * (part + 1)].rearrange("p t (c i) -> p c t i", i=4))
-            nc.vector.quantize_mx(out=zl_codes[part][:].bitcast(FP8X4), scales=zl_sc[part][:], in_=zi[:])
+        def weave_part(part, lo, hi, copy):
+            first = HALF * part
+            copy(zl[part][:, PACK * lo : PACK * hi].rearrange("p (c i t) -> p c t i", i=4, t=PACK), z_rows[1][:, :, first + lo : first + hi].rearrange("p t (c i) -> p c t i", i=4))
+
+        def quant_part(part, lo, hi):
+            nc.vector.quantize_mx(out=zl_codes[part][:, lo:hi].bitcast(FP8X4), scales=zl_sc[part][:, lo:hi], in_=zl[part][:, PACK * lo : PACK * hi])
 
         def stage2(part):
             for i in range(N // P):
@@ -237,17 +245,23 @@ def tile_list_fog_pair_yield_kernel(tc, tab_words, tab_scales, offs, pos1, pos2,
         root(1, 1)
         pick(2, 0, 0)
         pick(3, 0, 1)
-        times(2, 0)
-        times(3, 0)
+        times(2, 0, 0, HALF)
+        times(3, 0, 0, HALF)
         pick(3, 1, 0)
         pick(2, 1, 1)
-        root_part(2, 0)
-        root_part(3, 0)
-        times(3, 1)
-        times(2, 1)
-        quant_part(0, nc.scalar.copy)
-        root_part(3, 1)
-        root_part(2, 1)
-        quant_part(1, nc.vector.tensor_copy)
+        root_part(2, 0, 0, HALF)
+        root_part(3, 0, 0, HALF)
+        times(3, 1, 0, HALF)
+        times(2, 1, 0, P)
+        times(2, 1, P, HALF)
+        weave_part(0, 0, HALF, nc.scalar.copy)
+        quant_part(0, 0, HALF)
+        root_part(3, 1, 0, HALF)
+        root_part(2, 1, 0, P)
+        root_part(2, 1, P, HALF)
+        weave_part(1, 0, P, nc.vector.tensor_copy)
+        weave_part(1, P, HALF, nc.vector.tensor_copy)
+        quant_part(1, 0, P)
+        quant_part(1, P, HALF)
         stage2(0)
         stage2(1)

from contextlib import ExitStack

import concourse.mybir as mybir

K, T, S, H, NP, N = 1536, 4096, 1024, 1024, 512, 640
FLOPS = 2 * K * H * S + 2 * H * N * NP

F32 = mybir.dt.float32
BF16 = mybir.dt.bfloat16
I32 = mybir.dt.int32
U32 = mybir.dt.uint32
U16 = mybir.dt.uint16
U8 = mybir.dt.uint8
FP8X4 = mybir.dt.float8_e4m3fn_x4
FP4X4 = mybir.dt.float4_e2m1fn_x4
ACT = mybir.ActivationFunctionType
ALU = mybir.AluOpType

P = 128
PACK = 4
KP = P * PACK
A1 = K // KP
A2 = H // KP
BANK = 512


def tile_list_fog_pair_yield_kernel(tc, tab_words, tab_scales, offs, pos1, pos2, w1, gain, base, w2_words, w2_scales, thr, out):
    nc = tc.nc
    with ExitStack() as ctx:
        lists = ctx.enter_context(tc.tile_pool(name="lists", bufs=1))
        keep = ctx.enter_context(tc.tile_pool(name="keep", bufs=1))
        stage = ctx.enter_context(tc.tile_pool(name="stage", bufs=3))
        ring = ctx.enter_context(tc.tile_pool(name="ring", bufs=5))
        psum = ctx.enter_context(tc.psum_pool(name="psum", bufs=8))

        offs_t = lists.tile([P, S // 16], U16, name="offs_t")
        pos1_t = lists.tile([P, NP // 16], U16, name="pos1_t")
        pos2_t = lists.tile([P, NP // 16], U16, name="pos2_t")
        nc.sync.dma_start(offs_t[:], offs)

        sc_win = keep.tile([P, T], U8, name="sc_win", tag="slot01", align_bytes=64)
        for a in range(A1):
            nc.sync.dma_start(sc_win[16 + a : 64 : A1, :].bitcast(I32), tab_scales[a].bitcast(I32))
        nc.sync.dma_start(pos1_t[:], pos1)
        nc.sync.dma_start(pos2_t[:], pos2)
        nc.vector.memset(sc_win[0:16, :].bitcast(I32), 0)
        nc.vector.memset(sc_win[64:P, :].bitcast(I32), 0)

        warm_in = keep.tile([P, 1], F32, name="warm_in")
        warm_out = keep.tile([P, 1], F32, name="warm_out")
        nc.vector.memset(warm_in[:], 1.0)
        nc.scalar.activation(warm_out[:], warm_in[:], ACT.Sqrt)

        v_scales = keep.tile([P, A1 * S], U8, name="v_scales", align_bytes=64)
        nc.vector.memset(v_scales[:].bitcast(I32), 0)
        w2_sc = keep.tile([P, A2 * N], U8, name="w2_sc", align_bytes=64)
        nc.vector.memset(w2_sc[:].bitcast(I32), 0)

        gain_t = keep.tile([P, A2, PACK], F32, name="gain_t")
        base_t = keep.tile([P, A2, PACK], F32, name="base_t")
        thr_t = keep.tile([P, N // P], F32, name="thr_t")
        nc.gpsimd.dma_start(gain_t[:], gain.rearrange("(b p t) -> p b t", p=P, t=PACK))
        nc.gpsimd.dma_start(base_t[:], base.rearrange("(b p t) -> p b t", p=P, t=PACK))
        for q in range(4):
            nc.gpsimd.dma_start(
                w2_sc[32 * q : 32 * q + 4, :].bitcast(I32).rearrange("r (a c) -> r a c", a=A2),
                w2_scales[:, 4 * q : 4 * q + 4, :].rearrange("a r c -> r a c").bitcast(I32),
            )
        with nc.allow_non_contiguous_dma(reason="one threshold for each partition"):
            nc.gpsimd.dma_start(thr_t[:], thr.rearrange("(i p) -> p i", p=P))

        tab_win = [keep.tile([P, T], U16, name="tab_win", tag="slot_tab%d" % a, align_bytes=64) for a in range(A1)]
        v_words = [keep.tile([P, S], U16, name="v_words%d" % a, align_bytes=64) for a in range(A1)]
        w1_codes = {}
        w1_sc = {}
        raw = {}
        raw_slot = {(0, 0): "slot00", (0, 1): "slot01", (0, 2): "slot_tab0", (1, 0): "slot_tab1", (1, 1): "slot00", (1, 2): "slot_tab2"}

        def load_tab(a):
            nc.sync.dma_start(tab_win[a][:].bitcast(I32), tab_words[a].bitcast(I32))

        def load_w1(b, a):
            raw[b, a] = keep.tile([P, PACK, KP], F32, name="raw", tag=raw_slot[b, a], align_bytes=64)
            nc.sync.dma_start(raw[b, a][:], w1[KP * a : KP * (a + 1), KP * b : KP * (b + 1)].rearrange("(p j) c -> p j c", j=PACK))

        def quant_w1(b, a, m_vec, cuts=((0, KP),)):
            wb = stage.tile([P, PACK * KP], BF16, name="wb", align_bytes=64)
            dst = wb[:].rearrange("p (t m j) -> p m j t", t=PACK, j=PACK)
            src = raw[b, a][:].rearrange("p j (m t) -> p m j t", t=PACK)
            if m_vec < P:
                nc.scalar.copy(dst[:, m_vec:P], src[:, m_vec:P])
            if m_vec > 0:
                nc.vector.tensor_copy(dst[:, 0:m_vec], src[:, 0:m_vec])
            w1_codes[b, a] = keep.tile([P, KP], U32, name="w1_codes%d%d" % (b, a), align_bytes=64)
            w1_sc[b, a] = keep.tile([P, KP], U8, name="w1_sc%d%d" % (b, a), align_bytes=64)
            for lo, hi in cuts:
                nc.vector.quantize_mx(out=w1_codes[b, a][:, lo:hi].bitcast(FP8X4), scales=w1_sc[b, a][:, lo:hi], in_=wb[:, PACK * lo : PACK * hi])

        def gather_tab(a):
            nc.vector.tensor_copy(v_words[a][:], tab_win[a][:].indirect(offs_t[:]))

        load_tab(0)
        load_tab(1)
        load_w1(0, 0)
        load_tab(2)

        sc_got = keep.tile([P, S], U8, name="sc_got")
        nc.vector.tensor_copy(sc_got[:], sc_win[:].indirect(offs_t[:]))
        for q in range(4):
            nc.scalar.dma_start(
                v_scales[32 * q : 32 * q + 4, :].bitcast(I32).rearrange("r (a c) -> r a c", a=A1),
                sc_got[16 + 4 * A1 * q : 16 + 4 * A1 * (q + 1), :].bitcast(I32),
            )

        load_w1(0, 1)
        gather_tab(0)
        load_w1(0, 2)
        gather_tab(1)
        load_w1(1, 0)
        quant_w1(0, 0, 0)
        load_w1(1, 1)
        gather_tab(2)
        load_w1(1, 2)
        quant_w1(0, 1, 52)
        quant_w1(0, 2, 84, ((0, P), (P, 2 * P), (2 * P, KP)))

        h = {}

        def stage1(b, t):
            h[b, t] = keep.tile([P, S], F32, name="h%d%d" % (b, t))
            for half in range(S // BANK):
                cols = slice(BANK * half, BANK * (half + 1))
                acc = psum.tile([P, BANK], F32, name="acc", tag="acc")
                for a in range(A1):
                    nc.tensor.matmul_mx(
                        out=acc[:],
                        lhsT=w1_codes[b, a][:, P * t : P * (t + 1)].bitcast(FP8X4),
                        lhsT_scale=w1_sc[b, a][:, P * t : P * (t + 1)],
                        rhs=v_words[a][:, cols].bitcast(FP4X4),
                        rhs_scale=v_scales[:, S * a + BANK * half : S * a + BANK * (half + 1)],
                        start=(a == 0),
                        stop=(a == A1 - 1),
                    )
                nc.scalar.activation(h[b, t][:, cols], acc[:], ACT.Abs, scale=gain_t[:, b, t : t + 1])

        z_rows = [keep.tile([P, PACK, NP], BF16, name="z_rows%d" % b) for b in range(A2)]
        z_codes = [keep.tile([P, NP], U32, name="z_codes0", align_bytes=64)]
        z_sc = [keep.tile([P, NP], U8, name="z_sc0", align_bytes=64)]

        prods = {}

        def pairs(b, t):
            wind = ring.tile([P, NP], F32, name="wind")
            prods[b, t] = ring.tile([P, NP], F32, name="prod")
            parts = [(0, NP // 2), (NP // 2, NP)]
            for lo, hi in parts:
                nc.vector.tensor_copy(wind[:, lo:hi], h[b, t][:].indirect(pos1_t[:, lo // 16 : hi // 16]))
            for lo, hi in parts:
                nc.vector.tensor_tensor(prods[b, t][:, lo:hi], h[b, t][:].indirect(pos2_t[:, lo // 16 : hi // 16]), wind[:, lo:hi], ALU.mult)

        def root(b, t):
            nc.scalar.activation(z_rows[b][:, t, :], prods[b, t][:], ACT.Sqrt, bias=base_t[:, b, t : t + 1])

        def quant_z(b, copy):
            zi = stage.tile([P, NP * PACK], BF16, name="zi", align_bytes=64)
            copy(zi[:].rearrange("p (c i t) -> p c t i", i=4, t=PACK), z_rows[b][:].rearrange("p t (c i) -> p c t i", i=4))
            nc.vector.quantize_mx(out=z_codes[b][:].bitcast(FP8X4), scales=z_sc[b][:], in_=zi[:])

        stage1(0, 0)
        stage1(0, 1)
        pairs(0, 0)
        quant_w1(1, 0, 0)
        w2_t = keep.tile([P, A2, 2 * N], U8, name="w2_t", tag="slot01", align_bytes=64)
        nc.sync.dma_start(w2_t[:].bitcast(I32), w2_words.rearrange("a p c -> p a c").bitcast(I32))
        pairs(0, 1)
        stage1(0, 2)
        quant_w1(1, 1, 0)
        pairs(0, 2)
        quant_w1(1, 2, 64)
        stage1(0, 3)
        pairs(0, 3)
        root(0, 0)
        root(0, 1)
        stage1(1, 0)
        root(0, 2)
        pairs(1, 0)
        stage1(1, 1)
        root(0, 3)
        pairs(1, 1)
        stage1(1, 2)
        quant_z(0, nc.scalar.copy)
        root(1, 0)
        HALF = NP // 2
        wind_last = {}
        prod_last = {}

        def pick(t, part, slot):
            wind_last[t, part] = keep.tile([P, HALF], F32, name="wind_last", tag="wind_last%d" % slot)
            nc.vector.tensor_copy(wind_last[t, part][:], h[1, t][:].indirect(pos1_t[:, HALF // 16 * part : HALF // 16 * (part + 1)]))

            prod_last[t, part] = keep.tile([P, HALF], F32, name="prod_last%d%d" % (t, part))

        def times(t, part, lo, hi):
            first = HALF * part
            nc.vector.tensor_tensor(prod_last[t, part][:, lo:hi], h[1, t][:].indirect(pos2_t[:, (first + lo) // 16 : (first + hi) // 16]), wind_last[t, part][:, lo:hi], ALU.mult)

        def root_part(t, part, lo, hi):
            first = HALF * part
            nc.scalar.activation(z_rows[1][:, t, first + lo : first + hi], prod_last[t, part][:, lo:hi], ACT.Sqrt, bias=base_t[:, 1, t : t + 1])

        zl_codes = [keep.tile([P, HALF], U32, name="zl_codes%d" % part, align_bytes=64) for part in range(2)]
        zl_sc = [keep.tile([P, HALF], U8, name="zl_sc%d" % part, align_bytes=64) for part in range(2)]
        zl = [keep.tile([P, HALF * PACK], BF16, name="zl%d" % part, align_bytes=64) for part in range(2)]

        def weave_part(part, lo, hi, copy):
            first = HALF * part
            copy(zl[part][:, PACK * lo : PACK * hi].rearrange("p (c i t) -> p c t i", i=4, t=PACK), z_rows[1][:, :, first + lo : first + hi].rearrange("p t (c i) -> p c t i", i=4))

        def quant_part(part, lo, hi):
            nc.vector.quantize_mx(out=zl_codes[part][:, lo:hi].bitcast(FP8X4), scales=zl_sc[part][:, lo:hi], in_=zl[part][:, PACK * lo : PACK * hi])

        def stage2(part):
            for i in range(N // P):
                acc = psum.tile([P, BANK], F32, name="acc", tag="acc")
                for b in range(A2):
                    for c in range(HALF // P):
                        if b == 0:
                            codes, sc, lo = z_codes[0], z_sc[0], HALF * part + P * c
                        else:
                            codes, sc, lo = zl_codes[part], zl_sc[part], P * c
                        nc.tensor.matmul_mx(
                            out=acc[:, P * c : P * (c + 1)],
                            lhsT=w2_t[:, b, 2 * P * i : 2 * P * (i + 1)].bitcast(FP4X4),
                            lhsT_scale=w2_sc[:, N * b + P * i : N * b + P * (i + 1)],
                            rhs=codes[:, lo : lo + P].bitcast(FP8X4),
                            rhs_scale=sc[:, lo : lo + P],
                            start=(b == 0 and c == 0),
                            stop=(b == A2 - 1 and c == HALF // P - 1),
                        )
                res = keep.tile([P, HALF], F32, name="res%d%d" % (part, i))
                nc.scalar.activation(res[:], acc[:, 0:HALF], ACT.Abs, bias=thr_t[:, i : i + 1], scale=-1.0)
                nc.sync.dma_start(out[P * i : P * (i + 1), HALF * part : HALF * (part + 1)], res[:])

        stage1(1, 3)
        root(1, 1)
        pick(2, 0, 0)
        pick(3, 0, 1)
        times(2, 0, 0, HALF)
        times(3, 0, 0, HALF)
        pick(3, 1, 0)
        pick(2, 1, 1)
        root_part(2, 0, 0, HALF)
        root_part(3, 0, 0, HALF)
        times(3, 1, 0, HALF)
        times(2, 1, 0, P)
        times(2, 1, P, HALF)
        weave_part(0, 0, HALF, nc.scalar.copy)
        quant_part(0, 0, HALF)
        root_part(3, 1, 0, HALF)
        root_part(2, 1, 0, P)
        root_part(2, 1, P, HALF)
        weave_part(1, 0, P, nc.vector.tensor_copy)
        weave_part(1, P, HALF, nc.vector.tensor_copy)
        quant_part(1, 0, P)
        quant_part(1, P, HALF)
        stage2(0)
        stage2(1)
